import numpy as np
import ml_dtypes


def mxq(x, axis, fmt="e4m3"):
    dtype, down = {"e4m3": (ml_dtypes.float8_e4m3fn, 7), "e5m2": (ml_dtypes.float8_e5m2, 14)}[fmt]
    v = np.moveaxis(np.asarray(x, np.float32).astype(ml_dtypes.bfloat16).astype(np.float64), axis, -1)
    blocks = v.reshape(v.shape[:-1] + (-1, 32))
    amax = np.abs(blocks).max(-1, keepdims=True)
    byte = np.maximum(np.where(amax > 0, np.frexp(amax)[1] - 1 + 127, 0) - down, 1)
    scale = np.exp2(byte - 127.0)
    codes = (blocks / scale).astype(np.float32).astype(dtype).astype(np.float64)
    return np.moveaxis((codes * scale).reshape(v.shape), -1, axis)


WIDE = False


def mx_kscale(k):
    if not WIDE:
        return np.ones(k)
    levels = np.array([10, -10, 5, -5, 0])
    if k % 512:
        return np.exp2(np.random.permutation(np.resize(levels, k // 32))).repeat(32)
    a = np.empty((k // 512, 16))
    for p in range(k // 512):
        a[p, :8] = np.random.permutation(np.resize(levels, 8))
        for g in range(8):
            far = levels[np.abs(levels - a[p, g]) >= 10]
            a[p, g + 8] = far[np.random.randint(len(far))]
    return np.exp2(a.ravel()).repeat(32)


def f64(x):
    return np.asarray(x).astype(np.float64)


def striped(idx):
    return np.tile(idx.reshape(-1, 16).T, (8, 1)).astype(np.uint16)


def unstriped(offs):
    return offs[:16].T.reshape(-1).astype(np.int64)


def striped8(idx):
    return np.concatenate([x.reshape(-1, 16).T for x in idx]).astype(np.uint16)


def runs(offs, k):
    lists = np.stack([offs[16 * r : 16 * r + 16].T.reshape(-1) for r in range(8)]).astype(np.int64)
    return lists[np.arange(k) % 512 // 64]


def pack_weight(w):
    k, n = w.shape
    w = f64(np.asarray(w, np.float32).astype(ml_dtypes.bfloat16)).reshape(k // 32, 32, n)
    amax = np.abs(w).max(1)
    byte = np.clip(np.where(amax > 0, np.frexp(amax)[1] - 1 + 127 - 7, 1), 1, 254)
    scaled = (w * np.exp2(127.0 - byte)[:, None, :]).reshape(k, n).astype(np.float32)
    words = np.ascontiguousarray(scaled.reshape(k // 512, 128, 4, n).transpose(0, 1, 3, 2)).astype(ml_dtypes.float8_e4m3fn).view(np.uint8)
    return words, np.ascontiguousarray(byte.astype(np.uint8).reshape(k // 512, 16, n))


def unpack_weight(words, scales):
    g, p, n, _ = words.shape
    vals = np.ascontiguousarray(words).view(ml_dtypes.float8_e4m3fn).astype(np.float64) * np.repeat(np.exp2(scales.astype(np.float64) - 127.0), 8, axis=1)[..., None]
    return vals.transpose(0, 1, 3, 2).reshape(g * 512, n)


K, T, S, N, G, H = 512, 2048, 512, 512, 2048, 512


def setup_inputs():
    n = np.random.standard_normal
    s = mx_kscale(K)[:, None]
    u = mx_kscale(S)
    packed_xT = pack_weight(n((K, T)) * s)
    packed_dT = pack_weight(n((K, G)) / s)
    return {
        "x_words": packed_xT[0],
        "x_scales": packed_xT[1],
        "d_words": packed_dT[0],
        "d_scales": packed_dT[1],
        "gn": (np.random.uniform(0.5, 1.5, (H, 1)) * u[:, None]).astype(np.float32),
        "w1": (n((H, N)) / np.sqrt(H) / u[:, None]).astype(np.float32),
        "offs": striped(np.random.permutation(T)[:S]),
        "kidx": striped8(np.random.randint(0, G, (8, H))),
        "n1": striped8(np.stack([np.random.permutation(S) for _ in range(8)])),
        "n2": striped8(np.stack([np.random.permutation(S) for _ in range(8)])),
        "n3": striped8(np.stack([np.random.permutation(S) for _ in range(8)])),
        "n4": striped8(np.stack([np.random.permutation(S) for _ in range(8)])),
    }


def reference(x_words, x_scales, d_words, d_scales, gn, w1, offs, kidx, n1, n2, n3, n4):
    d_kidx = unpack_weight(d_words, d_scales)[np.arange(K)[:, None], runs(kidx, K)]
    xq = unpack_weight(x_words, x_scales)[:, unstriped(offs)]
    s = 0.0625 * (d_kidx.T @ xq)
    pa = s[np.arange(H)[:, None], runs(n1, H)]
    z = f64(gn) * ((2.0 * (s * pa)) / ((s) ** 2 + (pa) ** 2 + 0.5))
    h = mxq(f64(w1), 0, "e4m3").T @ mxq(z, 0, "e4m3")
    return 0.75 * (h * (h[np.arange(N)[:, None], runs(n2, N)]) + (h[np.arange(N)[:, None], runs(n3, N)]) * (h[np.arange(N)[:, None], runs(n4, N)]))

@@ -1,0 +1,160 @@
+from contextlib import ExitStack
+
+import concourse.mybir as mybir
+
+K, T, S, N, G, H = 512, 2048, 512, 512, 2048, 512
+FLOPS = 2 * K * H * S + 2 * H * N * S
+
+F32 = mybir.dt.float32
+BF16 = mybir.dt.bfloat16
+I32 = mybir.dt.int32
+U32 = mybir.dt.uint32
+U16 = mybir.dt.uint16
+U8 = mybir.dt.uint8
+FP8X4 = mybir.dt.float8_e4m3fn_x4
+ALU = mybir.AluOpType
+ACT = mybir.ActivationFunctionType
+
+P = 128
+PACK = 4
+CHUNKS = ((0, 256), (256, 128), (384, 128))
+
+
+def tile_picked_keyharmdot_none_p_kernel(
+    tc, x_words, x_scales, d_words, d_scales, gn, w1, offs, kidx, n1, n2, n3, n4, out
+):
+    nc = tc.nc
+    with ExitStack() as ctx:
+        keep = ctx.enter_context(tc.tile_pool(name="keep", bufs=1))
+        psum = ctx.enter_context(tc.psum_pool(name="psum", bufs=1))
+
+        def load_list(name, src):
+            t = keep.tile([P, S // 16], U16, name=name)
+            nc.sync.dma_start(t[:], src)
+            return t
+
+        warm = keep.tile([P, 8], F32, name="warm")
+        warm2 = keep.tile([P, 8], F32, name="warm2")
+        d_sc_tab = keep.tile([P, G], U8, name="d_sc_tab", tag="first", align_bytes=64)
+        x_sc_tab = keep.tile([P, T], U8, name="x_sc_tab", align_bytes=64)
+        nc.vector.memset(d_sc_tab[:].bitcast(I32), 0)
+        nc.vector.memset(x_sc_tab[:].bitcast(I32), 0)
+        nc.scalar.dma_start(d_sc_tab[0:P:8, :].bitcast(I32), d_scales[0].bitcast(I32))
+        nc.scalar.dma_start(x_sc_tab[0:P:8, :].bitcast(I32), x_scales[0].bitcast(I32))
+        nc.vector.memset(warm[:], 1.0)
+        nc.scalar.activation(warm2[:], warm[:], ACT.Abs_reciprocal_sqrt)
+
+        kidx_t = load_list("kidx_t", kidx)
+        offs_t = load_list("offs_t", offs)
+        d_tab = keep.tile([P, G], I32, name="d_tab", align_bytes=64)
+        nc.sync.dma_start(d_tab[:], d_words[0].rearrange("p n t -> p (n t)").bitcast(I32))
+        n1_t = load_list("n1_t", n1)
+        n2_t = load_list("n2_t", n2)
+        n3_t = load_list("n3_t", n3)
+        n4_t = load_list("n4_t", n4)
+        x_tab = keep.tile([P, T], I32, name="x_tab", align_bytes=64)
+        nc.sync.dma_start(x_tab[:], x_words[0].rearrange("p n t -> p (n t)").bitcast(I32))
+        gn_t = keep.tile([P, PACK], F32, name="gn_t")
+        nc.gpsimd.dma_start(gn_t[:], gn.rearrange("(p t) o -> p (t o)", t=PACK))
+
+        d_sc_g = keep.tile([P, H], U8, name="d_sc_g", align_bytes=64)
+        nc.vector.tensor_copy(d_sc_g[:], d_sc_tab[:].indirect(kidx_t[:]))
+        w_raw = keep.tile([P, PACK, N], F32, name="w_raw", tag="first", align_bytes=64)
+        nc.sync.dma_start(w_raw[:], w1.rearrange("(p j) m -> p j m", j=PACK))
+        x_sc_g = keep.tile([P, S], U8, name="x_sc_g", align_bytes=64)
+        nc.vector.tensor_copy(x_sc_g[:], x_sc_tab[:].indirect(offs_t[:]))
+        planes = keep.tile([P, H + S], U8, name="planes", align_bytes=64)
+        d_sc = planes[:, 0:H]
+        x_sc = planes[:, H : H + S]
+        nc.vector.tensor_copy(
+            d_sc.rearrange("p (t m) -> p m t", t=PACK), d_sc_g[:].rearrange("p (m t) -> p m t", t=PACK)
+        )
+        nc.vector.tensor_copy(x_sc.bitcast(I32), x_sc_g[:].bitcast(I32))
+        for m in range(1, 4):
+            nc.scalar.dma_start(planes[m:P:32, :].bitcast(I32), planes[8 * m : P : 32, :].bitcast(I32))
+        d_g = keep.tile([P, H], U32, name="d_g", align_bytes=64)
+        nc.vector.tensor_copy(d_g[:], d_tab[:].bitcast(U32).indirect(kidx_t[:]))
+        d_w = keep.tile([P, H], U32, name="d_w", align_bytes=64)
+        nc.vector.tensor_copy(
+            d_w[:].rearrange("p (t c i) -> p c t i", t=PACK, i=4), d_g[:].rearrange("p (c i t) -> p c t i", t=PACK, i=4)
+        )
+        x_w = keep.tile([P, S], U32, name="x_w", align_bytes=64)
+        nc.vector.tensor_copy(x_w[:], x_tab[:].bitcast(U32).indirect(offs_t[:]))
+
+        s_sb = []
+        s_sq = keep.tile([P, PACK, S], F32, name="s_sq")
+        s_banks = []
+        for t in range(PACK):
+            bank = psum.tile([P, S], F32, name="s_bank%d" % t)
+            cols = slice(t * P, (t + 1) * P)
+            nc.tensor.matmul_mx(
+                out=bank[:], lhsT=d_w[:, cols].bitcast(FP8X4), lhsT_scale=d_sc[:, cols],
+                rhs=x_w[:].bitcast(FP8X4), rhs_scale=x_sc, start=True, stop=True,
+            )
+            st = keep.tile([P, S], F32, name="s_sb%d" % t)
+            nc.scalar.activation(st[:], bank[:], ACT.Copy, scale=0.0625)
+            s_sb.append(st)
+            s_banks.append(bank)
+
+        w_bf = keep.tile([P, PACK * N], BF16, name="w_bf", align_bytes=64)
+        w_codes = keep.tile([P, N], U32, name="w_codes", align_bytes=64)
+        w_sc = keep.tile([P, N], U8, name="w_sc", align_bytes=64)
+
+        h_banks = [psum.tile([P, S], F32, name="h_bank%d" % t) for t in range(PACK)]
+        for ci, (c0, n) in enumerate(CHUNKS):
+            cols = slice(c0, c0 + n)
+            pa = keep.tile([P, PACK, n], F32, name="pa%d" % ci)
+            p2 = keep.tile([P, PACK, n], F32, name="p2%d" % ci)
+            den = keep.tile([P, PACK, n], F32, name="den%d" % ci)
+            num = keep.tile([P, PACK, n], F32, name="num%d" % ci)
+            rs = keep.tile([P, PACK, n], F32, name="rs%d" % ci)
+            r2 = keep.tile([P, PACK, n], F32, name="r2%d" % ci)
+            for t in range(PACK):
+                nc.vector.tensor_copy(pa[:, t, :], s_sb[t][:].indirect(n1_t[:, c0 // 16 : (c0 + n) // 16]))
+                nc.scalar.activation(s_sq[:, t, cols], s_banks[t][:, cols], ACT.Square, scale=0.0625)
+                nc.scalar.activation(p2[:, t, :], pa[:, t, :], ACT.Square)
+            for t in range(PACK):
+                nc.vector.scalar_tensor_tensor(den[:, t, :], p2[:, t, :], 0.5, s_sq[:, t, cols], ALU.add, ALU.add)
+                nc.vector.scalar_tensor_tensor(
+                    num[:, t, :], pa[:, t, :], gn_t[:, t : t + 1], s_sb[t][:, cols], ALU.mult, ALU.mult
+                )
+                nc.scalar.activation(rs[:, t, :], den[:, t, :], ACT.Abs_reciprocal_sqrt, scale=0.5)
+                nc.scalar.activation(r2[:, t, :], rs[:, t, :], ACT.Square)
+            if ci == 0:
+                nc.scalar.copy(
+                    w_bf[:].rearrange("p (t m j) -> p m j t", t=PACK, j=PACK),
+                    w_raw[:].rearrange("p j (m t) -> p m j t", t=PACK),
+                )
+                nc.vector.quantize_mx(out=w_codes[:].bitcast(FP8X4), scales=w_sc[:], in_=w_bf[:])
+            z_bf = keep.tile([P, n * PACK], BF16, name="z_bf%d" % ci, align_bytes=64)
+            nc.vector.tensor_tensor(
+                z_bf[:].rearrange("p (c i t) -> p c t i", t=PACK, i=4),
+                num[:].rearrange("p t (c i) -> p c t i", i=4),
+                r2[:].rearrange("p t (c i) -> p c t i", i=4),
+                ALU.mult,
+            )
+            z_codes = keep.tile([P, n], U32, name="z_codes%d" % ci, align_bytes=64)
+            z_sc = keep.tile([P, n], U8, name="z_sc%d" % ci, align_bytes=64)
+            nc.vector.quantize_mx(out=z_codes[:].bitcast(FP8X4), scales=z_sc[:], in_=z_bf[:])
+            for t in range(PACK):
+                wc = slice(t * P, (t + 1) * P)
+                nc.tensor.matmul_mx(
+                    out=h_banks[t][:, cols], lhsT=w_codes[:, wc].bitcast(FP8X4), lhsT_scale=w_sc[:, wc],
+                    rhs=z_codes[:].bitcast(FP8X4), rhs_scale=z_sc[:], start=True, stop=True,
+                )
+
+        out_rows = out.rearrange("(p t) j -> p t j", t=PACK)
+        for t in range(PACK):
+            h_win = keep.tile([P, 2 * S], F32, name="h_win%d" % t)
+            h_own = keep.tile([P, S], F32, name="h_own%d" % t)
+            nc.scalar.copy(h_win[:, 0:S], h_banks[t][:])
+            nc.scalar.activation(h_own[:], h_banks[t][:], ACT.Copy, scale=0.75)
+            b = keep.tile([P, S], F32, name="b%d" % t)
+            a = keep.tile([P, S], F32, name="a%d" % t)
+            c = keep.tile([P, S], F32, name="c%d" % t)
+            res = keep.tile([P, S], F32, name="res%d" % t)
+            nc.vector.tensor_scalar(b[:], h_win[:].indirect(n3_t[:]), 0.75, 0.0, ALU.mult, ALU.add)
+            nc.vector.tensor_tensor(a[:], h_win[:].indirect(n2_t[:]), h_own[:], ALU.mult)
+            nc.vector.tensor_tensor(c[:], h_win[:].indirect(n4_t[:]), b[:], ALU.mult)
+            nc.vector.tensor_tensor(res[:], a[:], c[:], ALU.add)
+            nc.sync.dma_start(out_rows[:, t, :], res[:])

@@ -1,6 +1,7 @@
 from contextlib import ExitStack
 
 import concourse.mybir as mybir
+from concourse.masks import make_identity
 
 K, T, S, N, G, H = 512, 2048, 512, 512, 2048, 512
 FLOPS = 2 * K * H * S + 2 * H * N * S
@@ -17,7 +18,8 @@ ACT = mybir.ActivationFunctionType
 
 P = 128
 PACK = 4
-CHUNKS = ((0, 256), (256, 128), (384, 128))
+CH = 128
+W_SPLIT = 40
 
 
 def tile_picked_keyharmdot_none_p_kernel(
@@ -33,34 +35,35 @@ def tile_picked_keyharmdot_none_p_kernel(
             nc.sync.dma_start(t[:], src)
             return t
 
-        warm = keep.tile([P, 8], F32, name="warm")
+        quarter = keep.tile([P, 8], F32, name="quarter")
         warm2 = keep.tile([P, 8], F32, name="warm2")
-        d_sc_tab = keep.tile([P, G], U8, name="d_sc_tab", tag="first", align_bytes=64)
+        d_sc_tab = keep.tile([P, G], U8, name="d_sc_tab", align_bytes=64)
         x_sc_tab = keep.tile([P, T], U8, name="x_sc_tab", align_bytes=64)
         nc.vector.memset(d_sc_tab[:].bitcast(I32), 0)
-        nc.vector.memset(x_sc_tab[:].bitcast(I32), 0)
-        nc.scalar.dma_start(d_sc_tab[0:P:8, :].bitcast(I32), d_scales[0].bitcast(I32))
-        nc.scalar.dma_start(x_sc_tab[0:P:8, :].bitcast(I32), x_scales[0].bitcast(I32))
-        nc.vector.memset(warm[:], 1.0)
-        nc.scalar.activation(warm2[:], warm[:], ACT.Abs_reciprocal_sqrt)
+        nc.gpsimd.memset(x_sc_tab[:].bitcast(I32), 0)
+        nc.vector.memset(quarter[:], 0.25)
+        nc.scalar.activation(warm2[:], quarter[:], ACT.Abs_reciprocal_sqrt)
+
+        ident = keep.tile([P, P], F32, name="ident")
+        make_identity(nc, ident[:])
 
         kidx_t = load_list("kidx_t", kidx)
+        nc.sync.dma_start(d_sc_tab[0:P:8, :].bitcast(I32), d_scales[0].bitcast(I32))
         offs_t = load_list("offs_t", offs)
-        d_tab = keep.tile([P, G], I32, name="d_tab", align_bytes=64)
-        nc.sync.dma_start(d_tab[:], d_words[0].rearrange("p n t -> p (n t)").bitcast(I32))
         n1_t = load_list("n1_t", n1)
+        gn_t = keep.tile([P, PACK], F32, name="gn_t")
+        nc.sync.dma_start(gn_t[:], gn.rearrange("(p t) o -> p (t o)", t=PACK))
+        nc.sync.dma_start(x_sc_tab[0:P:8, :].bitcast(I32), x_scales[0].bitcast(I32))
+        d_tab = keep.tile([P, G], I32, name="d_tab", tag="first", align_bytes=64)
+        nc.sync.dma_start(d_tab[:], d_words[0].rearrange("p n t -> p (n t)").bitcast(I32))
+        x_tab = keep.tile([P, T], I32, name="x_tab", align_bytes=64)
+        nc.sync.dma_start(x_tab[:], x_words[0].rearrange("p n t -> p (n t)").bitcast(I32))
         n2_t = load_list("n2_t", n2)
         n3_t = load_list("n3_t", n3)
         n4_t = load_list("n4_t", n4)
-        x_tab = keep.tile([P, T], I32, name="x_tab", align_bytes=64)
-        nc.sync.dma_start(x_tab[:], x_words[0].rearrange("p n t -> p (n t)").bitcast(I32))
-        gn_t = keep.tile([P, PACK], F32, name="gn_t")
-        nc.gpsimd.dma_start(gn_t[:], gn.rearrange("(p t) o -> p (t o)", t=PACK))
 
         d_sc_g = keep.tile([P, H], U8, name="d_sc_g", align_bytes=64)
         nc.vector.tensor_copy(d_sc_g[:], d_sc_tab[:].indirect(kidx_t[:]))
-        w_raw = keep.tile([P, PACK, N], F32, name="w_raw", tag="first", align_bytes=64)
-        nc.sync.dma_start(w_raw[:], w1.rearrange("(p j) m -> p j m", j=PACK))
         x_sc_g = keep.tile([P, S], U8, name="x_sc_g", align_bytes=64)
         nc.vector.tensor_copy(x_sc_g[:], x_sc_tab[:].indirect(offs_t[:]))
         planes = keep.tile([P, H + S], U8, name="planes", align_bytes=64)
@@ -74,6 +77,8 @@ def tile_picked_keyharmdot_none_p_kernel(
             nc.scalar.dma_start(planes[m:P:32, :].bitcast(I32), planes[8 * m : P : 32, :].bitcast(I32))
         d_g = keep.tile([P, H], U32, name="d_g", align_bytes=64)
         nc.vector.tensor_copy(d_g[:], d_tab[:].bitcast(U32).indirect(kidx_t[:]))
+        w_raw = keep.tile([P, PACK, N], F32, name="w_raw", tag="first", align_bytes=64)
+        nc.sync.dma_start(w_raw[:], w1.rearrange("(p j) m -> p j m", j=PACK))
         d_w = keep.tile([P, H], U32, name="d_w", align_bytes=64)
         nc.vector.tensor_copy(
             d_w[:].rearrange("p (t c i) -> p c t i", t=PACK, i=4), d_g[:].rearrange("p (c i t) -> p c t i", t=PACK, i=4)
@@ -81,8 +86,9 @@ def tile_picked_keyharmdot_none_p_kernel(
         x_w = keep.tile([P, S], U32, name="x_w", align_bytes=64)
         nc.vector.tensor_copy(x_w[:], x_tab[:].bitcast(U32).indirect(offs_t[:]))
 
-        s_sb = []
+        s_win = []
         s_sq = keep.tile([P, PACK, S], F32, name="s_sq")
+        pa = keep.tile([P, PACK, S], F32, name="pa")
         s_banks = []
         for t in range(PACK):
             bank = psum.tile([P, S], F32, name="s_bank%d" % t)
@@ -91,70 +97,134 @@ def tile_picked_keyharmdot_none_p_kernel(
                 out=bank[:], lhsT=d_w[:, cols].bitcast(FP8X4), lhsT_scale=d_sc[:, cols],
                 rhs=x_w[:].bitcast(FP8X4), rhs_scale=x_sc, start=True, stop=True,
             )
-            st = keep.tile([P, S], F32, name="s_sb%d" % t)
-            nc.scalar.activation(st[:], bank[:], ACT.Copy, scale=0.0625)
-            s_sb.append(st)
+            st = keep.tile([P, 2 * S], F32, name="s_win%d" % t)
+            nc.scalar.activation(st[:, 0:S], bank[:], ACT.Copy, scale=0.0625)
+            nc.vector.tensor_copy(pa[:, t, :], st[:].indirect(n1_t[:]))
+            s_win.append(st)
             s_banks.append(bank)
+        for t in range(PACK):
+            nc.scalar.activation(s_sq[:, t, :], s_banks[t][:], ACT.Square, scale=0.0625)
 
         w_bf = keep.tile([P, PACK * N], BF16, name="w_bf", align_bytes=64)
         w_codes = keep.tile([P, N], U32, name="w_codes", align_bytes=64)
         w_sc = keep.tile([P, N], U8, name="w_sc", align_bytes=64)
+        w_dst = w_bf[:].rearrange("p (t m j) -> p m j t", t=PACK, j=PACK)
+        w_src = w_raw[:].rearrange("p j (m t) -> p m j t", t=PACK)
+        nc.scalar.copy(w_dst[:, 0:W_SPLIT], w_src[:, 0:W_SPLIT])
+        nc.vector.tensor_copy(w_dst[:, W_SPLIT:P], w_src[:, W_SPLIT:P])
+        nc.vector.quantize_mx(out=w_codes[:].bitcast(FP8X4), scales=w_sc[:], in_=w_bf[:])
 
         h_banks = [psum.tile([P, S], F32, name="h_bank%d" % t) for t in range(PACK)]
-        for ci, (c0, n) in enumerate(CHUNKS):
-            cols = slice(c0, c0 + n)
-            pa = keep.tile([P, PACK, n], F32, name="pa%d" % ci)
-            p2 = keep.tile([P, PACK, n], F32, name="p2%d" % ci)
-            den = keep.tile([P, PACK, n], F32, name="den%d" % ci)
-            num = keep.tile([P, PACK, n], F32, name="num%d" % ci)
-            rs = keep.tile([P, PACK, n], F32, name="rs%d" % ci)
-            r2 = keep.tile([P, PACK, n], F32, name="r2%d" % ci)
+        h_wins = [keep.tile([P, 2 * S], F32, name="h_win%d" % t) for t in range(PACK)]
+        nch = S // CH
+        p2 = [keep.tile([P, PACK, CH], F32, name="p2%d" % ci) for ci in range(nch)]
+        den = {}
+        h_last = {}
+
+        for ci in range(nch - 1):
+            den[ci] = psum.tile([P, PACK, CH], F32, name="denT%d" % ci, tag="s_bank%d" % ci)
             for t in range(PACK):
-                nc.vector.tensor_copy(pa[:, t, :], s_sb[t][:].indirect(n1_t[:, c0 // 16 : (c0 + n) // 16]))
-                nc.scalar.activation(s_sq[:, t, cols], s_banks[t][:, cols], ACT.Square, scale=0.0625)
-                nc.scalar.activation(p2[:, t, :], pa[:, t, :], ACT.Square)
+                nc.tensor.matmul(
+                    den[ci][:, t, :], s_sq[:, t, ci * CH : (ci + 1) * CH], ident[:], start=(t == 0), stop=False, is_transpose=True
+                )
+
+        def front(ci):
+            cols = slice(ci * CH, (ci + 1) * CH)
+            nc.scalar.activation(p2[ci][:], pa[:, :, cols], ACT.Square)
+            if ci < nch - 1:
+                for t in range(PACK):
+                    nc.tensor.matmul(
+                        den[ci][:, t, :], p2[ci][:, t, :], ident[:], start=False, stop=(t == PACK - 1), is_transpose=True
+                    )
+            else:
+                den[ci] = keep.tile([P, PACK, CH], F32, name="den_last")
+                nc.vector.tensor_tensor(den[ci][:], p2[ci][:], s_sq[:, :, cols], ALU.add)
             for t in range(PACK):
-                nc.vector.scalar_tensor_tensor(den[:, t, :], p2[:, t, :], 0.5, s_sq[:, t, cols], ALU.add, ALU.add)
                 nc.vector.scalar_tensor_tensor(
-                    num[:, t, :], pa[:, t, :], gn_t[:, t : t + 1], s_sb[t][:, cols], ALU.mult, ALU.mult
+                    s_sq[:, t, cols], pa[:, t, cols], gn_t[:, t : t + 1], s_win[t][:, cols], ALU.mult, ALU.mult
                 )
-                nc.scalar.activation(rs[:, t, :], den[:, t, :], ACT.Abs_reciprocal_sqrt, scale=0.5)
-                nc.scalar.activation(r2[:, t, :], rs[:, t, :], ACT.Square)
-            if ci == 0:
-                nc.scalar.copy(
-                    w_bf[:].rearrange("p (t m j) -> p m j t", t=PACK, j=PACK),
-                    w_raw[:].rearrange("p j (m t) -> p m j t", t=PACK),
-                )
-                nc.vector.quantize_mx(out=w_codes[:].bitcast(FP8X4), scales=w_sc[:], in_=w_bf[:])
-            z_bf = keep.tile([P, n * PACK], BF16, name="z_bf%d" % ci, align_bytes=64)
+
+        def back(ci):
+            cols = slice(ci * CH, (ci + 1) * CH)
+            rs = keep.tile([P, PACK, CH], F32, name="rs%d" % ci)
+            r2 = keep.tile([P, PACK, CH], F32, name="r2%d" % ci)
+            nc.scalar.activation(rs[:], den[ci][:], ACT.Abs_reciprocal_sqrt, scale=0.5, bias=quarter[:, 0:1])
+            nc.scalar.activation(r2[:], rs[:], ACT.Square)
+            if ci < nch - 1:
+                r2t = r2
+                r2 = psum.tile([P, PACK, CH], F32, name="r2b%d" % ci, tag="s_bank%d" % ci)
+                for t in range(PACK):
+                    nc.tensor.transpose(r2[:, t, :], r2t[:, t, :], ident[:])
+            else:
+                h_last[0] = psum.tile([P, CH], F32, name="h_last", tag="s_bank3")
+            z_bf = keep.tile([P, CH * PACK], BF16, name="z_bf%d" % ci, align_bytes=64)
             nc.vector.tensor_tensor(
                 z_bf[:].rearrange("p (c i t) -> p c t i", t=PACK, i=4),
-                num[:].rearrange("p t (c i) -> p c t i", i=4),
+                s_sq[:, :, cols].rearrange("p t (c i) -> p c t i", i=4),
                 r2[:].rearrange("p t (c i) -> p c t i", i=4),
                 ALU.mult,
             )
-            z_codes = keep.tile([P, n], U32, name="z_codes%d" % ci, align_bytes=64)
-            z_sc = keep.tile([P, n], U8, name="z_sc%d" % ci, align_bytes=64)
+            z_codes = keep.tile([P, CH], U32, name="z_codes%d" % ci, align_bytes=64)
+            z_sc = keep.tile([P, CH], U8, name="z_sc%d" % ci, align_bytes=64)
             nc.vector.quantize_mx(out=z_codes[:].bitcast(FP8X4), scales=z_sc[:], in_=z_bf[:])
             for t in range(PACK):
                 wc = slice(t * P, (t + 1) * P)
+                dst = h_last[0][:] if (t == 0 and ci == nch - 1) else h_banks[t][:, cols]
                 nc.tensor.matmul_mx(
-                    out=h_banks[t][:, cols], lhsT=w_codes[:, wc].bitcast(FP8X4), lhsT_scale=w_sc[:, wc],
+                    out=dst, lhsT=w_codes[:, wc].bitcast(FP8X4), lhsT_scale=w_sc[:, wc],
                     rhs=z_codes[:].bitcast(FP8X4), rhs_scale=z_sc[:], start=True, stop=True,
                 )
 
+        front(0)
+        for ci in range(nch):
+            if ci + 1 < nch:
+                front(ci + 1)
+            back(ci)
+
         out_rows = out.rearrange("(p t) j -> p t j", t=PACK)
+        h_owns = []
         for t in range(PACK):
-            h_win = keep.tile([P, 2 * S], F32, name="h_win%d" % t)
+            h_win = h_wins[t]
             h_own = keep.tile([P, S], F32, name="h_own%d" % t)
-            nc.scalar.copy(h_win[:, 0:S], h_banks[t][:])
-            nc.scalar.activation(h_own[:], h_banks[t][:], ACT.Copy, scale=0.75)
+            if t == 0:
+                nc.scalar.copy(h_win[:, 0 : S - CH], h_banks[0][:, 0 : S - CH])
+                nc.vector.tensor_copy(h_win[:, S - CH : S], h_last[0][:])
+                nc.scalar.activation(h_own[:], h_win[:, 0:S], ACT.Copy, scale=0.75)
+            else:
+                nc.scalar.copy(h_win[:, 0:S], h_banks[t][:])
+                nc.scalar.activation(h_own[:], h_banks[t][:], ACT.Copy, scale=0.75)
+            h_owns.append(h_own)
+        for t in range(PACK):
+            h_win, h_own = h_wins[t], h_owns[t]
             b = keep.tile([P, S], F32, name="b%d" % t)
             a = keep.tile([P, S], F32, name="a%d" % t)
             c = keep.tile([P, S], F32, name="c%d" % t)
             res = keep.tile([P, S], F32, name="res%d" % t)
             nc.vector.tensor_scalar(b[:], h_win[:].indirect(n3_t[:]), 0.75, 0.0, ALU.mult, ALU.add)
             nc.vector.tensor_tensor(a[:], h_win[:].indirect(n2_t[:]), h_own[:], ALU.mult)
-            nc.vector.tensor_tensor(c[:], h_win[:].indirect(n4_t[:]), b[:], ALU.mult)
-            nc.vector.tensor_tensor(res[:], a[:], c[:], ALU.add)
-            nc.sync.dma_start(out_rows[:, t, :], res[:])
+            if t < PACK - 1:
+                nc.vector.tensor_tensor(c[:], h_win[:].indirect(n4_t[:]), b[:], ALU.mult)
+                sum_t = psum.tile([P, PACK, P], F32, name="sumT%d" % t, tag="s_bank%d" % (2 * (t % 2)))
+                for k, term in enumerate((a, c)):
+                    for g in range(PACK):
+                        nc.tensor.matmul(
+                            sum_t[:, g, :], term[:, g * P : (g + 1) * P], ident[:],
+                            start=(k == 0 and g == 0), stop=(k == 1 and g == PACK - 1), is_transpose=True,
+                        )
+                sum_sb = keep.tile([P, PACK, P], F32, name="sum_sb%d" % t)
+                nc.scalar.copy(sum_sb[:], sum_t[:])
+                back_t = psum.tile([P, PACK, P], F32, name="back%d" % t, tag="s_bank%d" % (1 + 2 * (t % 2)))
+                for g in range(PACK):
+                    nc.tensor.transpose(back_t[:, g, :], sum_sb[:, g, :], ident[:])
+                nc.scalar.copy(res[:], back_t[:].rearrange("p g m -> p (g m)"))
+                nc.sync.dma_start(out_rows[:, t, :], res[:])
+            else:
+                for half in range(2):
+                    hc = slice(half * S // 2, (half + 1) * S // 2)
+                    nc.vector.tensor_tensor(
+                        c[:, hc], h_win[:].indirect(n4_t[:, half * S // 32 : (half + 1) * S // 32]), b[:, hc], ALU.mult
+                    )
+                for half in range(2):
+                    hc = slice(half * S // 2, (half + 1) * S // 2)
+                    nc.vector.tensor_tensor(res[:, hc], a[:, hc], c[:, hc], ALU.add)
+                    nc.sync.dma_start(out_rows[:, t, hc], res[:, hc])

@@ -19,7 +19,6 @@ ACT = mybir.ActivationFunctionType
 P = 128
 PACK = 4
 CH = 128
-W_SPLIT = 40
 
 
 def tile_picked_keyharmdot_none_p_kernel(
@@ -40,8 +39,8 @@ def tile_picked_keyharmdot_none_p_kernel(
         d_sc_tab = keep.tile([P, G], U8, name="d_sc_tab", align_bytes=64)
         x_sc_tab = keep.tile([P, T], U8, name="x_sc_tab", align_bytes=64)
         nc.vector.memset(d_sc_tab[:].bitcast(I32), 0)
-        nc.gpsimd.memset(x_sc_tab[:].bitcast(I32), 0)
-        nc.vector.memset(quarter[:], 0.25)
+        nc.vector.memset(x_sc_tab[:].bitcast(I32), 0)
+        nc.gpsimd.memset(quarter[:], 0.25)
         nc.scalar.activation(warm2[:], quarter[:], ACT.Abs_reciprocal_sqrt)
 
         ident = keep.tile([P, P], F32, name="ident")
@@ -54,9 +53,9 @@ def tile_picked_keyharmdot_none_p_kernel(
         gn_t = keep.tile([P, PACK], F32, name="gn_t")
         nc.sync.dma_start(gn_t[:], gn.rearrange("(p t) o -> p (t o)", t=PACK))
         nc.sync.dma_start(x_sc_tab[0:P:8, :].bitcast(I32), x_scales[0].bitcast(I32))
-        d_tab = keep.tile([P, G], I32, name="d_tab", tag="first", align_bytes=64)
+        d_tab = keep.tile([P, G], I32, name="d_tab", tag="keys", align_bytes=64)
         nc.sync.dma_start(d_tab[:], d_words[0].rearrange("p n t -> p (n t)").bitcast(I32))
-        x_tab = keep.tile([P, T], I32, name="x_tab", align_bytes=64)
+        x_tab = keep.tile([P, T], I32, name="x_tab", tag="first", align_bytes=64)
         nc.sync.dma_start(x_tab[:], x_words[0].rearrange("p n t -> p (n t)").bitcast(I32))
         n2_t = load_list("n2_t", n2)
         n3_t = load_list("n3_t", n3)
@@ -77,14 +76,13 @@ def tile_picked_keyharmdot_none_p_kernel(
             nc.scalar.dma_start(planes[m:P:32, :].bitcast(I32), planes[8 * m : P : 32, :].bitcast(I32))
         d_g = keep.tile([P, H], U32, name="d_g", align_bytes=64)
         nc.vector.tensor_copy(d_g[:], d_tab[:].bitcast(U32).indirect(kidx_t[:]))
-        w_raw = keep.tile([P, PACK, N], F32, name="w_raw", tag="first", align_bytes=64)
+        w_raw = keep.tile([P, PACK, N], F32, name="w_raw", tag="keys", align_bytes=64)
         nc.sync.dma_start(w_raw[:], w1.rearrange("(p j) m -> p j m", j=PACK))
-        d_w = keep.tile([P, H], U32, name="d_w", align_bytes=64)
-        nc.vector.tensor_copy(
-            d_w[:].rearrange("p (t c i) -> p c t i", t=PACK, i=4), d_g[:].rearrange("p (c i t) -> p c t i", t=PACK, i=4)
-        )
         x_w = keep.tile([P, S], U32, name="x_w", align_bytes=64)
         nc.vector.tensor_copy(x_w[:], x_tab[:].bitcast(U32).indirect(offs_t[:]))
+        d_w = keep.tile([P, H], U32, name="d_w", tag="first", align_bytes=64)
+        for t in range(PACK):
+            nc.vector.tensor_copy(d_w[:, t * P : (t + 1) * P], d_g[:, t:H:PACK])
 
         s_win = []
         s_sq = keep.tile([P, PACK, S], F32, name="s_sq")
@@ -110,14 +108,13 @@ def tile_picked_keyharmdot_none_p_kernel(
         w_sc = keep.tile([P, N], U8, name="w_sc", align_bytes=64)
         w_dst = w_bf[:].rearrange("p (t m j) -> p m j t", t=PACK, j=PACK)
         w_src = w_raw[:].rearrange("p j (m t) -> p m j t", t=PACK)
-        nc.scalar.copy(w_dst[:, 0:W_SPLIT], w_src[:, 0:W_SPLIT])
-        nc.vector.tensor_copy(w_dst[:, W_SPLIT:P], w_src[:, W_SPLIT:P])
+        nc.vector.tensor_copy(w_dst, w_src)
         nc.vector.quantize_mx(out=w_codes[:].bitcast(FP8X4), scales=w_sc[:], in_=w_bf[:])
 
         h_banks = [psum.tile([P, S], F32, name="h_bank%d" % t) for t in range(PACK)]
         h_wins = [keep.tile([P, 2 * S], F32, name="h_win%d" % t) for t in range(PACK)]
         nch = S // CH
-        p2 = [keep.tile([P, PACK, CH], F32, name="p2%d" % ci) for ci in range(nch)]
+        p2 = keep.tile([P, PACK, S], F32, name="p2")
         den = {}
         h_last = {}
 
@@ -128,21 +125,18 @@ def tile_picked_keyharmdot_none_p_kernel(
                     den[ci][:, t, :], s_sq[:, t, ci * CH : (ci + 1) * CH], ident[:], start=(t == 0), stop=False, is_transpose=True
                 )
 
-        def front(ci):
-            cols = slice(ci * CH, (ci + 1) * CH)
-            nc.scalar.activation(p2[ci][:], pa[:, :, cols], ACT.Square)
-            if ci < nch - 1:
-                for t in range(PACK):
-                    nc.tensor.matmul(
-                        den[ci][:, t, :], p2[ci][:, t, :], ident[:], start=False, stop=(t == PACK - 1), is_transpose=True
-                    )
-            else:
-                den[ci] = keep.tile([P, PACK, CH], F32, name="den_last")
-                nc.vector.tensor_tensor(den[ci][:], p2[ci][:], s_sq[:, :, cols], ALU.add)
-            for t in range(PACK):
-                nc.vector.scalar_tensor_tensor(
-                    s_sq[:, t, cols], pa[:, t, cols], gn_t[:, t : t + 1], s_win[t][:, cols], ALU.mult, ALU.mult
+        for t in range(PACK):
+            nc.scalar.activation(p2[:, t, :], pa[:, t, :], ACT.Square)
+            for ci in range(nch - 1):
+                nc.tensor.matmul(
+                    den[ci][:, t, :], p2[:, t, ci * CH : (ci + 1) * CH], ident[:], start=False, stop=(t == PACK - 1), is_transpose=True
                 )
+        den[nch - 1] = keep.tile([P, PACK, CH], F32, name="den_last")
+        nc.vector.tensor_tensor(den[nch - 1][:], p2[:, :, S - CH : S], s_sq[:, :, S - CH : S], ALU.add)
+        for t in range(PACK):
+            nc.vector.scalar_tensor_tensor(
+                p2[:, t, :], pa[:, t, :], gn_t[:, t : t + 1], s_win[t][:, 0:S], ALU.mult, ALU.mult
+            )
 
         def back(ci):
             cols = slice(ci * CH, (ci + 1) * CH)
@@ -160,26 +154,27 @@ def tile_picked_keyharmdot_none_p_kernel(
             z_bf = keep.tile([P, CH * PACK], BF16, name="z_bf%d" % ci, align_bytes=64)
             nc.vector.tensor_tensor(
                 z_bf[:].rearrange("p (c i t) -> p c t i", t=PACK, i=4),
-                s_sq[:, :, cols].rearrange("p t (c i) -> p c t i", i=4),
+                p2[:, :, cols].rearrange("p t (c i) -> p c t i", i=4),
                 r2[:].rearrange("p t (c i) -> p c t i", i=4),
                 ALU.mult,
             )
-            z_codes = keep.tile([P, CH], U32, name="z_codes%d" % ci, align_bytes=64)
-            z_sc = keep.tile([P, CH], U8, name="z_sc%d" % ci, align_bytes=64)
-            nc.vector.quantize_mx(out=z_codes[:].bitcast(FP8X4), scales=z_sc[:], in_=z_bf[:])
-            for t in range(PACK):
-                wc = slice(t * P, (t + 1) * P)
-                dst = h_last[0][:] if (t == 0 and ci == nch - 1) else h_banks[t][:, cols]
-                nc.tensor.matmul_mx(
-                    out=dst, lhsT=w_codes[:, wc].bitcast(FP8X4), lhsT_scale=w_sc[:, wc],
-                    rhs=z_codes[:].bitcast(FP8X4), rhs_scale=z_sc[:], start=True, stop=True,
-                )
+            nc.vector.quantize_mx(out=z_codes[:, cols].bitcast(FP8X4), scales=z_sc[:, cols], in_=z_bf[:])
+            nc.tensor.matmul_mx(
+                out=h_last[0][:] if ci == nch - 1 else h_banks[0][:, cols],
+                lhsT=w_codes[:, 0:P].bitcast(FP8X4), lhsT_scale=w_sc[:, 0:P],
+                rhs=z_codes[:, cols].bitcast(FP8X4), rhs_scale=z_sc[:, cols], start=True, stop=True,
+            )
 
-        front(0)
+        z_codes = keep.tile([P, S], U32, name="z_codes", align_bytes=64)
+        z_sc = keep.tile([P, S], U8, name="z_sc", align_bytes=64)
         for ci in range(nch):
-            if ci + 1 < nch:
-                front(ci + 1)
             back(ci)
+        for t in range(1, PACK):
+            wc = slice(t * P, (t + 1) * P)
+            nc.tensor.matmul_mx(
+                out=h_banks[t][:], lhsT=w_codes[:, wc].bitcast(FP8X4), lhsT_scale=w_sc[:, wc],
+                rhs=z_codes[:].bitcast(FP8X4), rhs_scale=z_sc[:], start=True, stop=True,
+            )
 
         out_rows = out.rearrange("(p t) j -> p t j", t=PACK)
         h_owns = []
@@ -217,7 +212,7 @@ def tile_picked_keyharmdot_none_p_kernel(
                 for g in range(PACK):
                     nc.tensor.transpose(back_t[:, g, :], sum_sb[:, g, :], ident[:])
                 nc.scalar.copy(res[:], back_t[:].rearrange("p g m -> p (g m)"))
-                nc.sync.dma_start(out_rows[:, t, :], res[:])
+                nc.scalar.dma_start(out_rows[:, t, :], res[:])
             else:
                 for half in range(2):
                     hc = slice(half * S // 2, (half + 1) * S // 2)

from contextlib import ExitStack

import concourse.mybir as mybir
from concourse.masks import make_identity

K, T, S, N, G, H = 512, 2048, 512, 512, 2048, 512
FLOPS = 2 * K * H * S + 2 * H * N * S

F32 = mybir.dt.float32
BF16 = mybir.dt.bfloat16
I32 = mybir.dt.int32
U32 = mybir.dt.uint32
U16 = mybir.dt.uint16
U8 = mybir.dt.uint8
FP8X4 = mybir.dt.float8_e4m3fn_x4
ALU = mybir.AluOpType
ACT = mybir.ActivationFunctionType

P = 128
PACK = 4
CH = 128


def tile_picked_keyharmdot_none_p_kernel(
    tc, x_words, x_scales, d_words, d_scales, gn, w1, offs, kidx, n1, n2, n3, n4, out
):
    nc = tc.nc
    with ExitStack() as ctx:
        keep = ctx.enter_context(tc.tile_pool(name="keep", bufs=1))
        psum = ctx.enter_context(tc.psum_pool(name="psum", bufs=1))

        def load_list(name, src):
            t = keep.tile([P, S // 16], U16, name=name)
            nc.sync.dma_start(t[:], src)
            return t

        quarter = keep.tile([P, 8], F32, name="quarter")
        warm2 = keep.tile([P, 8], F32, name="warm2")
        d_sc_tab = keep.tile([P, G], U8, name="d_sc_tab", align_bytes=64)
        x_sc_tab = keep.tile([P, T], U8, name="x_sc_tab", align_bytes=64)
        nc.vector.memset(d_sc_tab[:].bitcast(I32), 0)
        nc.vector.memset(x_sc_tab[:].bitcast(I32), 0)
        nc.gpsimd.memset(quarter[:], 0.25)
        nc.scalar.activation(warm2[:], quarter[:], ACT.Abs_reciprocal_sqrt)

        ident = keep.tile([P, P], F32, name="ident")
        make_identity(nc, ident[:])

        kidx_t = load_list("kidx_t", kidx)
        nc.sync.dma_start(d_sc_tab[0:P:8, :].bitcast(I32), d_scales[0].bitcast(I32))
        offs_t = load_list("offs_t", offs)
        n1_t = load_list("n1_t", n1)
        gn_t = keep.tile([P, PACK], F32, name="gn_t")
        nc.sync.dma_start(gn_t[:], gn.rearrange("(p t) o -> p (t o)", t=PACK))
        nc.sync.dma_start(x_sc_tab[0:P:8, :].bitcast(I32), x_scales[0].bitcast(I32))
        d_tab = keep.tile([P, G], I32, name="d_tab", tag="keys", align_bytes=64)
        nc.sync.dma_start(d_tab[:], d_words[0].rearrange("p n t -> p (n t)").bitcast(I32))
        x_tab = keep.tile([P, T], I32, name="x_tab", tag="first", align_bytes=64)
        nc.sync.dma_start(x_tab[:], x_words[0].rearrange("p n t -> p (n t)").bitcast(I32))
        n2_t = load_list("n2_t", n2)
        n3_t = load_list("n3_t", n3)
        n4_t = load_list("n4_t", n4)

        d_sc_g = keep.tile([P, H], U8, name="d_sc_g", align_bytes=64)
        nc.vector.tensor_copy(d_sc_g[:], d_sc_tab[:].indirect(kidx_t[:]))
        x_sc_g = keep.tile([P, S], U8, name="x_sc_g", align_bytes=64)
        nc.vector.tensor_copy(x_sc_g[:], x_sc_tab[:].indirect(offs_t[:]))
        planes = keep.tile([P, H + S], U8, name="planes", align_bytes=64)
        d_sc = planes[:, 0:H]
        x_sc = planes[:, H : H + S]
        nc.vector.tensor_copy(
            d_sc.rearrange("p (t m) -> p m t", t=PACK), d_sc_g[:].rearrange("p (m t) -> p m t", t=PACK)
        )
        nc.vector.tensor_copy(x_sc.bitcast(I32), x_sc_g[:].bitcast(I32))
        for m in range(1, 4):
            nc.scalar.dma_start(planes[m:P:32, :].bitcast(I32), planes[8 * m : P : 32, :].bitcast(I32))
        d_g = keep.tile([P, H], U32, name="d_g", align_bytes=64)
        nc.vector.tensor_copy(d_g[:], d_tab[:].bitcast(U32).indirect(kidx_t[:]))
        w_raw = keep.tile([P, PACK, N], F32, name="w_raw", tag="keys", align_bytes=64)
        nc.sync.dma_start(w_raw[:], w1.rearrange("(p j) m -> p j m", j=PACK))
        x_w = keep.tile([P, S], U32, name="x_w", align_bytes=64)
        nc.vector.tensor_copy(x_w[:], x_tab[:].bitcast(U32).indirect(offs_t[:]))
        d_w = keep.tile([P, H], U32, name="d_w", tag="first", align_bytes=64)
        for t in range(PACK):
            nc.vector.tensor_copy(d_w[:, t * P : (t + 1) * P], d_g[:, t:H:PACK])

        s_win = []
        s_sq = keep.tile([P, PACK, S], F32, name="s_sq")
        pa = keep.tile([P, PACK, S], F32, name="pa")
        s_banks = []
        for t in range(PACK):
            bank = psum.tile([P, S], F32, name="s_bank%d" % t)
            cols = slice(t * P, (t + 1) * P)
            nc.tensor.matmul_mx(
                out=bank[:], lhsT=d_w[:, cols].bitcast(FP8X4), lhsT_scale=d_sc[:, cols],
                rhs=x_w[:].bitcast(FP8X4), rhs_scale=x_sc, start=True, stop=True,
            )
            st = keep.tile([P, 2 * S], F32, name="s_win%d" % t)
            nc.scalar.activation(st[:, 0:S], bank[:], ACT.Copy, scale=0.0625)
            nc.vector.tensor_copy(pa[:, t, :], st[:].indirect(n1_t[:]))
            s_win.append(st)
            s_banks.append(bank)
        for t in range(PACK):
            nc.scalar.activation(s_sq[:, t, :], s_banks[t][:], ACT.Square, scale=0.0625)

        w_bf = keep.tile([P, PACK * N], BF16, name="w_bf", align_bytes=64)
        w_codes = keep.tile([P, N], U32, name="w_codes", align_bytes=64)
        w_sc = keep.tile([P, N], U8, name="w_sc", align_bytes=64)
        w_dst = w_bf[:].rearrange("p (t m j) -> p m j t", t=PACK, j=PACK)
        w_src = w_raw[:].rearrange("p j (m t) -> p m j t", t=PACK)
        nc.vector.tensor_copy(w_dst, w_src)
        nc.vector.quantize_mx(out=w_codes[:].bitcast(FP8X4), scales=w_sc[:], in_=w_bf[:])

        h_banks = [psum.tile([P, S], F32, name="h_bank%d" % t) for t in range(PACK)]
        h_wins = [keep.tile([P, 2 * S], F32, name="h_win%d" % t) for t in range(PACK)]
        nch = S // CH
        p2 = keep.tile([P, PACK, S], F32, name="p2")
        den = {}
        h_last = {}

        for ci in range(nch - 1):
            den[ci] = psum.tile([P, PACK, CH], F32, name="denT%d" % ci, tag="s_bank%d" % ci)
            for t in range(PACK):
                nc.tensor.matmul(
                    den[ci][:, t, :], s_sq[:, t, ci * CH : (ci + 1) * CH], ident[:], start=(t == 0), stop=False, is_transpose=True
                )

        for t in range(PACK):
            nc.scalar.activation(p2[:, t, :], pa[:, t, :], ACT.Square)
            for ci in range(nch - 1):
                nc.tensor.matmul(
                    den[ci][:, t, :], p2[:, t, ci * CH : (ci + 1) * CH], ident[:], start=False, stop=(t == PACK - 1), is_transpose=True
                )
        den[nch - 1] = keep.tile([P, PACK, CH], F32, name="den_last")
        nc.vector.tensor_tensor(den[nch - 1][:], p2[:, :, S - CH : S], s_sq[:, :, S - CH : S], ALU.add)
        for t in range(PACK):
            nc.vector.scalar_tensor_tensor(
                p2[:, t, :], pa[:, t, :], gn_t[:, t : t + 1], s_win[t][:, 0:S], ALU.mult, ALU.mult
            )

        def back(ci):
            cols = slice(ci * CH, (ci + 1) * CH)
            rs = keep.tile([P, PACK, CH], F32, name="rs%d" % ci)
            r2 = keep.tile([P, PACK, CH], F32, name="r2%d" % ci)
            nc.scalar.activation(rs[:], den[ci][:], ACT.Abs_reciprocal_sqrt, scale=0.5, bias=quarter[:, 0:1])
            nc.scalar.activation(r2[:], rs[:], ACT.Square)
            if ci < nch - 1:
                r2t = r2
                r2 = psum.tile([P, PACK, CH], F32, name="r2b%d" % ci, tag="s_bank%d" % ci)
                for t in range(PACK):
                    nc.tensor.transpose(r2[:, t, :], r2t[:, t, :], ident[:])
            else:
                h_last[0] = psum.tile([P, CH], F32, name="h_last", tag="s_bank3")
            z_bf = keep.tile([P, CH * PACK], BF16, name="z_bf%d" % ci, align_bytes=64)
            nc.vector.tensor_tensor(
                z_bf[:].rearrange("p (c i t) -> p c t i", t=PACK, i=4),
                p2[:, :, cols].rearrange("p t (c i) -> p c t i", i=4),
                r2[:].rearrange("p t (c i) -> p c t i", i=4),
                ALU.mult,
            )
            nc.vector.quantize_mx(out=z_codes[:, cols].bitcast(FP8X4), scales=z_sc[:, cols], in_=z_bf[:])
            nc.tensor.matmul_mx(
                out=h_last[0][:] if ci == nch - 1 else h_banks[0][:, cols],
                lhsT=w_codes[:, 0:P].bitcast(FP8X4), lhsT_scale=w_sc[:, 0:P],
                rhs=z_codes[:, cols].bitcast(FP8X4), rhs_scale=z_sc[:, cols], start=True, stop=True,
            )

        z_codes = keep.tile([P, S], U32, name="z_codes", align_bytes=64)
        z_sc = keep.tile([P, S], U8, name="z_sc", align_bytes=64)
        for ci in range(nch):
            back(ci)
        for t in range(1, PACK):
            wc = slice(t * P, (t + 1) * P)
            nc.tensor.matmul_mx(
                out=h_banks[t][:], lhsT=w_codes[:, wc].bitcast(FP8X4), lhsT_scale=w_sc[:, wc],
                rhs=z_codes[:].bitcast(FP8X4), rhs_scale=z_sc[:], start=True, stop=True,
            )

        out_rows = out.rearrange("(p t) j -> p t j", t=PACK)
        h_owns = []
        for t in range(PACK):
            h_win = h_wins[t]
            h_own = keep.tile([P, S], F32, name="h_own%d" % t)
            if t == 0:
                nc.scalar.copy(h_win[:, 0 : S - CH], h_banks[0][:, 0 : S - CH])
                nc.vector.tensor_copy(h_win[:, S - CH : S], h_last[0][:])
                nc.scalar.activation(h_own[:], h_win[:, 0:S], ACT.Copy, scale=0.75)
            else:
                nc.scalar.copy(h_win[:, 0:S], h_banks[t][:])
                nc.scalar.activation(h_own[:], h_banks[t][:], ACT.Copy, scale=0.75)
            h_owns.append(h_own)
        for t in range(PACK):
            h_win, h_own = h_wins[t], h_owns[t]
            b = keep.tile([P, S], F32, name="b%d" % t)
            a = keep.tile([P, S], F32, name="a%d" % t)
            c = keep.tile([P, S], F32, name="c%d" % t)
            res = keep.tile([P, S], F32, name="res%d" % t)
            nc.vector.tensor_scalar(b[:], h_win[:].indirect(n3_t[:]), 0.75, 0.0, ALU.mult, ALU.add)
            nc.vector.tensor_tensor(a[:], h_win[:].indirect(n2_t[:]), h_own[:], ALU.mult)
            if t < PACK - 1:
                nc.vector.tensor_tensor(c[:], h_win[:].indirect(n4_t[:]), b[:], ALU.mult)
                sum_t = psum.tile([P, PACK, P], F32, name="sumT%d" % t, tag="s_bank%d" % (2 * (t % 2)))
                for k, term in enumerate((a, c)):
                    for g in range(PACK):
                        nc.tensor.matmul(
                            sum_t[:, g, :], term[:, g * P : (g + 1) * P], ident[:],
                            start=(k == 0 and g == 0), stop=(k == 1 and g == PACK - 1), is_transpose=True,
                        )
                sum_sb = keep.tile([P, PACK, P], F32, name="sum_sb%d" % t)
                nc.scalar.copy(sum_sb[:], sum_t[:])
                back_t = psum.tile([P, PACK, P], F32, name="back%d" % t, tag="s_bank%d" % (1 + 2 * (t % 2)))
                for g in range(PACK):
                    nc.tensor.transpose(back_t[:, g, :], sum_sb[:, g, :], ident[:])
                nc.scalar.copy(res[:], back_t[:].rearrange("p g m -> p (g m)"))
                nc.scalar.dma_start(out_rows[:, t, :], res[:])
            else:
                for half in range(2):
                    hc = slice(half * S // 2, (half + 1) * S // 2)
                    nc.vector.tensor_tensor(
                        c[:, hc], h_win[:].indirect(n4_t[:, half * S // 32 : (half + 1) * S // 32]), b[:, hc], ALU.mult
                    )
                for half in range(2):
                    hc = slice(half * S // 2, (half + 1) * S // 2)
                    nc.vector.tensor_tensor(res[:, hc], a[:, hc], c[:, hc], ALU.add)
                    nc.sync.dma_start(out_rows[:, t, hc], res[:, hc])
